import numpy as np
import ml_dtypes


def mxq(x, axis, fmt="e4m3"):
    dtype, down = {"e4m3": (ml_dtypes.float8_e4m3fn, 7), "e5m2": (ml_dtypes.float8_e5m2, 14)}[fmt]
    v = np.moveaxis(np.asarray(x, np.float32).astype(ml_dtypes.bfloat16).astype(np.float64), axis, -1)
    blocks = v.reshape(v.shape[:-1] + (-1, 32))
    amax = np.abs(blocks).max(-1, keepdims=True)
    byte = np.maximum(np.where(amax > 0, np.frexp(amax)[1] - 1 + 127, 0) - down, 1)
    scale = np.exp2(byte - 127.0)
    codes = (blocks / scale).astype(np.float32).astype(dtype).astype(np.float64)
    return np.moveaxis((codes * scale).reshape(v.shape), -1, axis)


WIDE = False


def mx_kscale(k):
    if not WIDE:
        return np.ones(k)
    levels = np.array([10, -10, 5, -5, 0])
    if k % 512:
        return np.exp2(np.random.permutation(np.resize(levels, k // 32))).repeat(32)
    a = np.empty((k // 512, 16))
    for p in range(k // 512):
        a[p, :8] = np.random.permutation(np.resize(levels, 8))
        for g in range(8):
            far = levels[np.abs(levels - a[p, g]) >= 10]
            a[p, g + 8] = far[np.random.randint(len(far))]
    return np.exp2(a.ravel()).repeat(32)


def f64(x):
    return np.asarray(x).astype(np.float64)


def striped(idx):
    return np.tile(idx.reshape(-1, 16).T, (8, 1)).astype(np.uint16)


def unstriped(offs):
    return offs[:16].T.reshape(-1).astype(np.int64)


E2M1 = np.array([0.0, 0.5, 1.0, 1.5, 2.0, 3.0, 4.0, 6.0, -0.0, -0.5, -1.0, -1.5, -2.0, -3.0, -4.0, -6.0])


def pack_weight(w, fmt):
    k, n = w.shape
    w = f64(np.asarray(w, np.float32).astype(ml_dtypes.bfloat16)).reshape(k // 32, 32, n)
    amax = np.abs(w).max(1)
    if fmt == "e4m3":
        byte = np.frexp(amax)[1] - 1 + 127 - 7
    else:
        mant, ex = np.frexp(amax / 6.0)
        byte = np.where(mant > 0.5, ex, ex - 1) + 127
    byte = np.clip(np.where(amax > 0, byte, 1), 1, 254)
    scaled = (w * np.exp2(127.0 - byte)[:, None, :]).reshape(k, n).astype(np.float32)
    by_word = np.ascontiguousarray(scaled.reshape(k // 512, 128, 4, n).transpose(0, 1, 3, 2))
    if fmt == "e4m3":
        words = by_word.astype(ml_dtypes.float8_e4m3fn).view(np.uint8)
    else:
        c = by_word.astype(ml_dtypes.float4_e2m1fn).view(np.uint8) & 0xF
        words = (c[..., 0::2] | (c[..., 1::2] << 4)).reshape(k // 512, 128, 2 * n)
    return np.ascontiguousarray(words), np.ascontiguousarray(byte.astype(np.uint8).reshape(k // 512, 16, n))


def unpack_weight(words, scales, fmt):
    g, _, n = scales.shape
    words = np.ascontiguousarray(words).reshape(g, 128, n, -1)
    if fmt == "e4m3":
        vals = words.view(ml_dtypes.float8_e4m3fn).astype(np.float64)
    else:
        nib = np.empty((g, 128, n, 4), np.uint8)
        nib[..., 0::2] = words & 0xF
        nib[..., 1::2] = words >> 4
        vals = E2M1[nib]
    vals = vals * np.repeat(np.exp2(scales.astype(np.float64) - 127.0), 8, axis=1)[..., None]
    return vals.transpose(0, 1, 3, 2).reshape(g * 512, n)


def gelu(v):
    return 0.5 * v * (1.0 + np.tanh(np.sqrt(2.0 / np.pi) * (v + 0.044715 * v**3)))


K, K2, H, N, T, TB, S, P = 1024, 512, 1024, 512, 4096, 2048, 1024, 512

def setup_inputs():
    n = np.random.standard_normal
    s, s2, u = mx_kscale(K)[:, None], mx_kscale(K2)[:, None], mx_kscale(H)[:, None]
    d = {}
    d["tab_words"], d["tab_scales"] = pack_weight(n((K, T)) * s, "e4m3")
    d["tab2_words"], d["tab2_scales"] = pack_weight(n((K2, TB)) * s2, "e4m3")
    d["offs"] = striped(np.random.permutation(T)[:S])
    d["offs2"] = striped(np.random.permutation(TB)[:P])
    d["pos1"] = striped(np.random.permutation(S)[:P])
    d["w1"] = (1.5 * n((K, H)) / s / K ** 0.5).astype(np.float32)
    d["w2_words"], d["w2_scales"] = pack_weight(1.8 * n((K2, H)) / s2 * u.T / K2 ** 0.5, "e2m1")
    d["bias"] = (0.9 * n(H) * u[:, 0]).astype(np.float32)
    d["wgs"] = np.exp(0.3 * n((128, P))).astype(np.float32)
    d["gain"] = (0.6 * np.exp(0.3 * n(H)) * u[:, 0]).astype(np.float32)
    d["w3"] = (n((H, N)) / u / H ** 0.5).astype(np.float32)
    return d

def reference(tab_words, tab_scales, tab2_words, tab2_scales, offs, offs2, pos1, w1, w2_words, w2_scales, bias, wgs, gain, w3):
    v = unpack_weight(tab_words, tab_scales, "e4m3")[:, unstriped(offs)]
    v2 = unpack_weight(tab2_words, tab2_scales, "e4m3")[:, unstriped(offs2)]
    y1 = mxq(f64(w1), 0, "e4m3").T @ v
    a = np.sqrt(1.0 + np.square(y1))
    w2 = unpack_weight(w2_words, w2_scales, "e2m1")
    b = (w2.T @ v2) + f64(bias)[:, None]
    placed = np.zeros((H, S))
    placed[:, unstriped(pos1)] = np.tile(f64(wgs), (H // 128, 1)) * b
    z = placed / a + f64(gain)[:, None] * a
    return mxq(f64(w3), 0, "e4m3").T @ mxq(z, 0, "e4m3")

@@ -1,0 +1,258 @@
+from contextlib import ExitStack
+
+import concourse.mybir as mybir
+
+K, K2, H, N, T, TB, S, PL = 1024, 512, 1024, 512, 4096, 2048, 1024, 512
+FLOPS = 2 * (K * H * S + K2 * H * PL + H * N * S)
+
+F32 = mybir.dt.float32
+BF16 = mybir.dt.bfloat16
+I32 = mybir.dt.int32
+U32 = mybir.dt.uint32
+U16 = mybir.dt.uint16
+U8 = mybir.dt.uint8
+FP8X4 = mybir.dt.float8_e4m3fn_x4
+FP4X4 = mybir.dt.float4_e2m1fn_x4
+ALU = mybir.AluOpType
+ACT = mybir.ActivationFunctionType
+
+P = 128
+PACK = 4
+PASS = P * PACK
+HALF = 512
+EARLY = 3
+
+
+def tile_list_melt_track_porosity_kernel(
+    tc, tab_words, tab_scales, tab2_words, tab2_scales, offs, offs2, pos1,
+    w1, w2_words, w2_scales, bias, wgs, gain, w3, out,
+):
+    nc = tc.nc
+    with ExitStack() as ctx:
+        lists = ctx.enter_context(tc.tile_pool(name="lists", bufs=1))
+        keep = ctx.enter_context(tc.tile_pool(name="keep", bufs=1))
+        ring2 = ctx.enter_context(tc.tile_pool(name="ring2", bufs=2))
+        ring3 = ctx.enter_context(tc.tile_pool(name="ring3", bufs=3))
+        psum = ctx.enter_context(tc.psum_pool(name="psum", bufs=8))
+
+        def kept(shape, dtype, name, tag=None):
+            return keep.tile(shape, dtype, name=name, tag=tag or name, align_bytes=64)
+
+        offs_sb = lists.tile([P, S // 16], U16, name="offs_sb")
+        offs2_sb = lists.tile([P, PL // 16], U16, name="offs2_sb")
+        pos1_sb = lists.tile([P, PL // 16], U16, name="pos1_sb")
+
+        tabw = [kept([P, T], I32, "tabw%d" % a) for a in range(2)]
+        tabs = kept([P, T], U8, "tabs")
+        tab2w = kept([P, TB], I32, "tab2w")
+        tab2s = kept([P, TB], U8, "tab2s")
+        w2w_raw = kept([P, 2 * H], U8, "w2w_raw")
+        w2s_raw = kept([P, H], U8, "w2s_raw")
+        w2w = kept([P, 2 * H], U8, "w2w")
+        w2s = kept([P, H], U8, "w2s")
+        wgs0 = kept([P, 1, PL], F32, "wgs0")
+        wgs1 = kept([P, 1, PL], F32, "wgs1")
+        wgs23 = kept([P, 2, PL], F32, "wgs23")
+        wgs_rows = wgs.rearrange("(m t) j -> m t j", t=PACK)
+        bias_sb = kept([P, 2, PACK], F32, "bias_sb")
+        gain_sb = kept([P, 2, PACK], F32, "gain_sb")
+        pages = [kept([P, S], F32, "page%d" % i) for i in range(2)]
+        warm = kept([P, 2], F32, "warm")
+
+        nc.vector.memset(w2s_raw[:].bitcast(I32), 0)
+        nc.vector.memset(tab2s[:].bitcast(I32), 0)
+        nc.vector.memset(warm[:], 1.0)
+        nc.gpsimd.memset(tabs[:].bitcast(I32), 0)
+        for page in pages:
+            nc.gpsimd.memset(page[:], 0.0)
+        nc.scalar.activation(warm[:, 1:2], warm[:, 0:1], ACT.Abs_reciprocal_sqrt)
+
+        nc.sync.dma_start(offs2_sb[:], offs2)
+        nc.sync.dma_start(w2w_raw[:].bitcast(I32), w2_words[0].bitcast(I32))
+        nc.sync.dma_start(tab2w[:], tab2_words[0].rearrange("p t i -> p (t i)").bitcast(I32))
+        for q in range(4):
+            nc.sync.dma_start(w2s_raw[32 * q : 32 * q + 4, :].bitcast(I32), w2_scales[0, 4 * q : 4 * q + 4, :].bitcast(I32))
+        for q in range(4):
+            nc.sync.dma_start(tab2s[32 * q : 32 * q + 4, :].bitcast(I32), tab2_scales[0, 4 * q : 4 * q + 4, :].bitcast(I32))
+        nc.sync.dma_start(pos1_sb[:], pos1)
+        nc.sync.dma_start(bias_sb[:], bias.rearrange("(g p t) -> p g t", g=2, t=PACK))
+
+        def load_wgs(tile, t0, t1):
+            for q in (0, 2, 1, 3):
+                nc.sync.dma_start(tile[32 * q : 32 * q + 32], wgs_rows[:, t0:t1, :])
+
+        load_wgs(wgs0, 0, 1)
+
+        def load_table(a):
+            nc.sync.dma_start(tabw[a][:], tab_words[a].rearrange("p t i -> p (t i)").bitcast(I32))
+
+        def load_rows(rows, name):
+            raw = ring3.tile([P, PACK, HALF], F32, name=name, tag="raw")
+            nc.sync.dma_start(raw[:], rows.rearrange("(p j) c -> p j c", j=PACK))
+            return raw
+
+        def quantise(grouped, name, width=HALF):
+            codes = kept([P, width], U32, name + "_codes")
+            scales = kept([P, width], U8, name + "_scales")
+            nc.vector.quantize_mx(out=codes[:].bitcast(FP8X4), scales=scales[:], in_=grouped[:])
+            return codes, scales
+
+        def prepare_w1(a, g):
+            raw = load_rows(w1[PASS * a : PASS * (a + 1), PASS * g : PASS * (g + 1)], "w1raw")
+            grouped = ring2.tile([P, PACK * HALF], BF16, name="grouped", tag="grouped", align_bytes=64)
+            nc.scalar.copy(
+                grouped[:].rearrange("p (t m j) -> p m j t", t=PACK, j=PACK),
+                raw[:].rearrange("p j (m t) -> p m j t", t=PACK),
+            )
+            return quantise(grouped, "w1_%d%d" % (a, g))
+
+        def prepare_w3(g):
+            raw = load_rows(w3[PASS * g : PASS * (g + 1), :], "w3raw")
+            grouped = ring2.tile([P, PACK * HALF], BF16, name="grouped", tag="grouped", align_bytes=64)
+            nc.scalar.copy(
+                grouped[:].rearrange("p (c i t) -> p c t i", t=PACK, i=4),
+                raw[:].rearrange("p t (c i) -> p c t i", i=4),
+            )
+            return quantise(grouped, "w3_%d" % g)
+
+        nc.vector.tensor_copy(
+            w2w[:].bitcast(U16).rearrange("p (g t m) -> p g t m", g=2, t=PACK),
+            w2w_raw[:].bitcast(U16).rearrange("p (g m t) -> p g t m", g=2, t=PACK),
+        )
+        nc.vector.tensor_copy(
+            w2s[:].rearrange("p (g t m) -> p g t m", g=2, t=PACK),
+            w2s_raw[:].rearrange("p (g m t) -> p g t m", g=2, t=PACK),
+        )
+        v2 = kept([P, PL], U32, "v2")
+        v2s = kept([P, PL], U8, "v2s")
+        nc.vector.tensor_copy(v2[:], tab2w[:].bitcast(U32).indirect(offs2_sb[:]))
+        nc.vector.tensor_copy(v2s[:], tab2s[:].indirect(offs2_sb[:]))
+
+        b_sb = kept([P, 2 * PACK, PL], F32, "b_sb")
+        order = (0, 4, 1, 5, 2, 3, 6, 7)
+        for n in order:
+            g, t = divmod(n, PACK)
+            bank = psum.tile([P, PL], F32, name="bank_b", tag="bank")
+            nc.tensor.matmul_mx(
+                out=bank[:],
+                lhsT=w2w[:, 2 * P * n : 2 * P * (n + 1)].bitcast(FP4X4),
+                lhsT_scale=w2s[:, P * n : P * (n + 1)],
+                rhs=v2[:].bitcast(FP8X4),
+                rhs_scale=v2s[:],
+                start=True,
+                stop=True,
+            )
+            nc.scalar.activation(b_sb[:, n, :], bank[:], ACT.Identity, bias=bias_sb[:, g, t : t + 1])
+
+        for name in ("tab2w", "w2w_raw", "tab2s", "w2s_raw", "v2", "w2w"):
+            page = kept([P, S], F32, "page_" + name, tag=name)
+            nc.gpsimd.memset(page[:], 0.0)
+            pages.append(page)
+        page_of = {n: pages[i] for i, n in enumerate(order)}
+
+        def place(n):
+            t = n % PACK
+            weight = (wgs0[:, 0, :], wgs1[:, 0, :], wgs23[:, 0, :], wgs23[:, 1, :])[t]
+            nc.vector.tensor_tensor(page_of[n][:].indirect(pos1_sb[:]), b_sb[:, n, :], weight, ALU.mult)
+
+        place(0)
+        place(4)
+
+        load_table(0)
+        nc.sync.dma_start(offs_sb[:], offs)
+        for q in range(4):
+            nc.sync.dma_start(tabs[32 * q : 32 * q + 8, :].bitcast(I32), tab_scales[:, 4 * q : 4 * q + 4, :].bitcast(I32))
+        nc.sync.dma_start(gain_sb[:], gain.rearrange("(g p t) -> p g t", g=2, t=PACK))
+        v0 = kept([P, S], U32, "v0")
+        vs = kept([P, S], U8, "vs")
+        nc.vector.tensor_copy(v0[:], tabw[0][:].bitcast(U32).indirect(offs_sb[:]))
+        nc.vector.tensor_copy(vs[:], tabs[:].indirect(offs_sb[:]))
+        w1q = {}
+        for a in range(2):
+            w1q[a, 0] = prepare_w1(a, 0)
+        load_table(1)
+        v1 = [kept([P, HALF], U32, "v1_%d" % h) for h in range(2)]
+        for h in range(2):
+            nc.vector.tensor_copy(v1[h][:], tabw[1][:].bitcast(U32).indirect(offs_sb[:, 32 * h : 32 * (h + 1)]))
+
+        load_wgs(wgs1, 1, 2)
+        for a in range(2):
+            w1q[a, 1] = prepare_w1(a, 1)
+        w3q = [prepare_w3(0)]
+        load_wgs(wgs23, 2, 4)
+
+        def features(g, h, width=HALF):
+            cols = slice(HALF * h, HALF * (h + 1))
+            rs = ring3.tile([P, PACK, HALF], F32, name="rs", tag="rs")
+            u = ring3.tile([P, PACK, HALF], F32, name="u", tag="u")
+            sq = kept([P, PACK, HALF], F32, "sq", tag="tabw1")
+            for t in range(PACK):
+                bank = psum.tile([P, HALF], F32, name="bank_y", tag="bank")
+                for a in range(2):
+                    codes, scales = w1q[a, g]
+                    moving = v0[:, cols] if a == 0 else v1[h][:]
+                    nc.tensor.matmul_mx(
+                        out=bank[:],
+                        lhsT=codes[:, P * t : P * (t + 1)].bitcast(FP8X4),
+                        lhsT_scale=scales[:, P * t : P * (t + 1)],
+                        rhs=moving.bitcast(FP8X4),
+                        rhs_scale=vs[4 * a : P, cols],
+                        start=(a == 0),
+                        stop=(a == 1),
+                    )
+                gain_col = gain_sb[:, g, t : t + 1]
+                nc.scalar.activation(sq[:, t, :], bank[:], ACT.Square)
+                nc.scalar.activation(u[:, t, :], sq[:, t, :], ACT.Identity, bias=gain_col, scale=gain_col)
+                nc.vector.tensor_tensor(u[:, t, :], u[:, t, :], page_of[PACK * g + t][:, cols], ALU.add)
+            nc.scalar.activation(rs[:], sq[:], ACT.Abs_reciprocal_sqrt, bias=1.0)
+            pieces = []
+            for c0 in range(0, HALF, width):
+                z = ring2.tile([P, PACK * width], BF16, name="z", tag="z", align_bytes=64)
+                nc.vector.tensor_tensor(
+                    z[:].rearrange("p (c i t) -> p c t i", t=PACK, i=2),
+                    u[:, :, c0 : c0 + width].rearrange("p t (c i) -> p c t i", i=2),
+                    rs[:, :, c0 : c0 + width].rearrange("p t (c i) -> p c t i", i=2),
+                    ALU.mult,
+                )
+                pieces.append(quantise(z, "z_%d%d_%d" % (g, h, c0), width))
+            return pieces
+
+        out_rows = out.rearrange("(nt p) j -> p nt j", p=P)
+
+        def project(c0, width, zq, flat, last):
+            banks = [psum.tile([P, width], F32, name="bank_o", tag="bank") for nt in range(N // P)]
+            for g in range(2):
+                codes, scales = zq[g]
+                for nt in range(N // P):
+                    nc.tensor.matmul_mx(
+                        out=banks[nt][:],
+                        lhsT=w3q[g][0][:, P * nt : P * (nt + 1)].bitcast(FP8X4),
+                        lhsT_scale=w3q[g][1][:, P * nt : P * (nt + 1)],
+                        rhs=codes.bitcast(FP8X4),
+                        rhs_scale=scales,
+                        start=(g == 0),
+                        stop=(g == 1),
+                    )
+            for nt in range(N // P):
+                res = flat[:, width * nt : width * (nt + 1)]
+                if last and nt >= 2:
+                    nc.vector.tensor_copy(res, banks[nt][:])
+                else:
+                    nc.scalar.copy(res, banks[nt][:])
+                if nt % 2 == 1:
+                    pair = flat[:, width * (nt - 1) : width * (nt + 1)]
+                    nc.sync.dma_start(out_rows[:, nt - 1 : nt + 1, c0 : c0 + width], pair.rearrange("p (a b) -> p a b", a=2))
+
+        for n in (1, 5, 2, 3, 6, 7):
+            place(n)
+        z00 = features(0, 0)[0]
+        z01 = features(0, 1)[0]
+        w3q.append(prepare_w3(1))
+        z10 = features(1, 0)[0]
+        z11 = features(1, 1, HALF // 2)
+        staged0 = kept([P, PACK * HALF], F32, "staged0", tag="tabw1")
+        staged1 = kept([P, 2, PACK * 256], F32, "staged1", tag="tabw0")
+        project(0, HALF, ((z00[0][:], z00[1][:]), (z10[0][:], z10[1][:])), staged0[:], False)
+        for k in range(2):
+            cols = slice(256 * k, 256 * (k + 1))
+            project(HALF + 256 * k, 256, ((z01[0][:, cols], z01[1][:, cols]), (z11[k][0][:], z11[k][1][:])), staged1[:, k, :], k == 1)

@@ -56,26 +56,24 @@ def tile_list_melt_track_porosity_kernel(
         wgs_rows = wgs.rearrange("(m t) j -> m t j", t=PACK)
         bias_sb = kept([P, 2, PACK], F32, "bias_sb")
         gain_sb = kept([P, 2, PACK], F32, "gain_sb")
-        pages = [kept([P, S], F32, "page%d" % i) for i in range(2)]
+        pages = []
         warm = kept([P, 2], F32, "warm")
 
         nc.vector.memset(w2s_raw[:].bitcast(I32), 0)
-        nc.vector.memset(tab2s[:].bitcast(I32), 0)
+        nc.gpsimd.memset(tab2s[:].bitcast(I32), 0)
         nc.vector.memset(warm[:], 1.0)
         nc.gpsimd.memset(tabs[:].bitcast(I32), 0)
-        for page in pages:
-            nc.gpsimd.memset(page[:], 0.0)
         nc.scalar.activation(warm[:, 1:2], warm[:, 0:1], ACT.Abs_reciprocal_sqrt)
 
         nc.sync.dma_start(offs2_sb[:], offs2)
         nc.sync.dma_start(w2w_raw[:].bitcast(I32), w2_words[0].bitcast(I32))
-        nc.sync.dma_start(tab2w[:], tab2_words[0].rearrange("p t i -> p (t i)").bitcast(I32))
+        nc.sync.dma_start(bias_sb[:], bias.rearrange("(g p t) -> p g t", g=2, t=PACK))
         for q in range(4):
             nc.sync.dma_start(w2s_raw[32 * q : 32 * q + 4, :].bitcast(I32), w2_scales[0, 4 * q : 4 * q + 4, :].bitcast(I32))
+        nc.sync.dma_start(tab2w[:], tab2_words[0].rearrange("p t i -> p (t i)").bitcast(I32))
         for q in range(4):
             nc.sync.dma_start(tab2s[32 * q : 32 * q + 4, :].bitcast(I32), tab2_scales[0, 4 * q : 4 * q + 4, :].bitcast(I32))
         nc.sync.dma_start(pos1_sb[:], pos1)
-        nc.sync.dma_start(bias_sb[:], bias.rearrange("(g p t) -> p g t", g=2, t=PACK))
 
         def load_wgs(tile, t0, t1):
             for q in (0, 2, 1, 3):
@@ -100,10 +98,11 @@ def tile_list_melt_track_porosity_kernel(
         def prepare_w1(a, g):
             raw = load_rows(w1[PASS * a : PASS * (a + 1), PASS * g : PASS * (g + 1)], "w1raw")
             grouped = ring2.tile([P, PACK * HALF], BF16, name="grouped", tag="grouped", align_bytes=64)
-            nc.scalar.copy(
-                grouped[:].rearrange("p (t m j) -> p m j t", t=PACK, j=PACK),
-                raw[:].rearrange("p j (m t) -> p m j t", t=PACK),
-            )
+            for pair in range(2):
+                nc.scalar.copy(
+                    grouped[:].rearrange("p (t m j) -> p m j t", t=PACK, j=PACK)[:, :, :, 2 * pair : 2 * pair + 2],
+                    raw[:].rearrange("p j (m t) -> p m j t", t=PACK)[:, :, :, 2 * pair : 2 * pair + 2],
+                )
             return quantise(grouped, "w1_%d%d" % (a, g))
 
         def prepare_w3(g):
@@ -144,7 +143,7 @@ def tile_list_melt_track_porosity_kernel(
             )
             nc.scalar.activation(b_sb[:, n, :], bank[:], ACT.Identity, bias=bias_sb[:, g, t : t + 1])
 
-        for name in ("tab2w", "w2w_raw", "tab2s", "w2s_raw", "v2", "w2w"):
+        for name in ("w2w_raw", "w2s_raw", "tab2w", "tab2s", "v2", "w2w", "w2s", "v2s"):
             page = kept([P, S], F32, "page_" + name, tag=name)
             nc.gpsimd.memset(page[:], 0.0)
             pages.append(page)
@@ -162,29 +161,26 @@ def tile_list_melt_track_porosity_kernel(
         nc.sync.dma_start(offs_sb[:], offs)
         for q in range(4):
             nc.sync.dma_start(tabs[32 * q : 32 * q + 8, :].bitcast(I32), tab_scales[:, 4 * q : 4 * q + 4, :].bitcast(I32))
-        nc.sync.dma_start(gain_sb[:], gain.rearrange("(g p t) -> p g t", g=2, t=PACK))
+        load_wgs(wgs1, 1, 2)
         v0 = kept([P, S], U32, "v0")
         vs = kept([P, S], U8, "vs")
         nc.vector.tensor_copy(v0[:], tabw[0][:].bitcast(U32).indirect(offs_sb[:]))
         nc.vector.tensor_copy(vs[:], tabs[:].indirect(offs_sb[:]))
         w1q = {}
-        for a in range(2):
-            w1q[a, 0] = prepare_w1(a, 0)
+        for g in range(2):
+            for a in range(2):
+                w1q[a, g] = prepare_w1(a, g)
+        place(1)
+        place(5)
         load_table(1)
+        nc.sync.dma_start(gain_sb[:], gain.rearrange("(g p t) -> p g t", g=2, t=PACK))
         v1 = [kept([P, HALF], U32, "v1_%d" % h) for h in range(2)]
         for h in range(2):
             nc.vector.tensor_copy(v1[h][:], tabw[1][:].bitcast(U32).indirect(offs_sb[:, 32 * h : 32 * (h + 1)]))
-
-        load_wgs(wgs1, 1, 2)
-        for a in range(2):
-            w1q[a, 1] = prepare_w1(a, 1)
-        w3q = [prepare_w3(0)]
         load_wgs(wgs23, 2, 4)
 
-        def features(g, h, width=HALF):
+        def features(g, h, u, rs):
             cols = slice(HALF * h, HALF * (h + 1))
-            rs = ring3.tile([P, PACK, HALF], F32, name="rs", tag="rs")
-            u = ring3.tile([P, PACK, HALF], F32, name="u", tag="u")
             sq = kept([P, PACK, HALF], F32, "sq", tag="tabw1")
             for t in range(PACK):
                 bank = psum.tile([P, HALF], F32, name="bank_y", tag="bank")
@@ -203,19 +199,21 @@ def tile_list_melt_track_porosity_kernel(
                 gain_col = gain_sb[:, g, t : t + 1]
                 nc.scalar.activation(sq[:, t, :], bank[:], ACT.Square)
                 nc.scalar.activation(u[:, t, :], sq[:, t, :], ACT.Identity, bias=gain_col, scale=gain_col)
+            nc.scalar.activation(rs, sq[:], ACT.Abs_reciprocal_sqrt, bias=1.0)
+
+        def add_placed(g, u, cols):
+            for t in range(PACK):
                 nc.vector.tensor_tensor(u[:, t, :], u[:, t, :], page_of[PACK * g + t][:, cols], ALU.add)
-            nc.scalar.activation(rs[:], sq[:], ACT.Abs_reciprocal_sqrt, bias=1.0)
-            pieces = []
-            for c0 in range(0, HALF, width):
-                z = ring2.tile([P, PACK * width], BF16, name="z", tag="z", align_bytes=64)
-                nc.vector.tensor_tensor(
-                    z[:].rearrange("p (c i t) -> p c t i", t=PACK, i=2),
-                    u[:, :, c0 : c0 + width].rearrange("p t (c i) -> p c t i", i=2),
-                    rs[:, :, c0 : c0 + width].rearrange("p t (c i) -> p c t i", i=2),
-                    ALU.mult,
-                )
-                pieces.append(quantise(z, "z_%d%d_%d" % (g, h, c0), width))
-            return pieces
+
+        def quantise_z(u, rs, width, name, tag):
+            z = keep.tile([P, PACK * width], BF16, name="z", tag=tag, align_bytes=64)
+            nc.vector.tensor_tensor(
+                z[:].rearrange("p (c i t) -> p c t i", t=PACK, i=4),
+                u.rearrange("p t (c i) -> p c t i", i=4),
+                rs.rearrange("p t (c i) -> p c t i", i=4),
+                ALU.mult,
+            )
+            return quantise(z, name, width)
 
         out_rows = out.rearrange("(nt p) j -> p nt j", p=P)
 
@@ -243,16 +241,30 @@ def tile_list_melt_track_porosity_kernel(
                     pair = flat[:, width * (nt - 1) : width * (nt + 1)]
                     nc.sync.dma_start(out_rows[:, nt - 1 : nt + 1, c0 : c0 + width], pair.rearrange("p (a b) -> p a b", a=2))
 
-        for n in (1, 5, 2, 3, 6, 7):
+        for n in (2, 3, 6, 7):
             place(n)
-        z00 = features(0, 0)[0]
-        z01 = features(0, 1)[0]
-        w3q.append(prepare_w3(1))
-        z10 = features(1, 0)[0]
-        z11 = features(1, 1, HALF // 2)
+        u0 = kept([P, PACK, S], F32, "u0")
+        rs0 = kept([P, PACK, S], F32, "rs0", tag="tabw0")
+        for h in range(2):
+            cols = slice(HALF * h, HALF * (h + 1))
+            features(0, h, u0[:, :, cols], rs0[:, :, cols])
+        add_placed(0, u0[:], slice(0, S))
+        z0 = quantise_z(u0[:], rs0[:], S, "z0", "z0")
+        w3q = [prepare_w3(g) for g in range(2)]
+        u1 = [kept([P, PACK, HALF], F32, "u1_%d" % h) for h in range(2)]
+        rs1 = [kept([P, PACK, HALF], F32, "rs1_%d" % h) for h in range(2)]
+        features(1, 0, u1[0][:], rs1[0][:])
+        add_placed(1, u1[0][:], slice(0, HALF))
+        z10 = quantise_z(u1[0][:], rs1[0][:], HALF, "z10", "z1")
+        features(1, 1, u1[1][:], rs1[1][:])
+        add_placed(1, u1[1][:], slice(HALF, S))
         staged0 = kept([P, PACK * HALF], F32, "staged0", tag="tabw1")
         staged1 = kept([P, 2, PACK * 256], F32, "staged1", tag="tabw0")
-        project(0, HALF, ((z00[0][:], z00[1][:]), (z10[0][:], z10[1][:])), staged0[:], False)
+        z11 = []
         for k in range(2):
             cols = slice(256 * k, 256 * (k + 1))
-            project(HALF + 256 * k, 256, ((z01[0][:, cols], z01[1][:, cols]), (z11[k][0][:], z11[k][1][:])), staged1[:, k, :], k == 1)
+            z11.append(quantise_z(u1[1][:, :, cols], rs1[1][:, :, cols], 256, "z11_%d" % k, ("z0", "z1")[k]))
+        project(0, HALF, ((z0[0][:, 0:HALF], z0[1][:, 0:HALF]), (z10[0][:], z10[1][:])), staged0[:], False)
+        for k in range(2):
+            cols = slice(HALF + 256 * k, HALF + 256 * (k + 1))
+            project(HALF + 256 * k, 256, ((z0[0][:, cols], z0[1][:, cols]), (z11[k][0][:], z11[k][1][:])), staged1[:, k, :], k == 1)

@@ -1,6 +1,7 @@
 from contextlib import ExitStack
 
 import concourse.mybir as mybir
+from concourse.masks import make_identity
 
 K, K2, H, N, T, TB, S, PL = 1024, 512, 1024, 512, 4096, 2048, 1024, 512
 FLOPS = 2 * (K * H * S + K2 * H * PL + H * N * S)
@@ -31,8 +32,8 @@ def tile_list_melt_track_porosity_kernel(
     with ExitStack() as ctx:
         lists = ctx.enter_context(tc.tile_pool(name="lists", bufs=1))
         keep = ctx.enter_context(tc.tile_pool(name="keep", bufs=1))
-        ring2 = ctx.enter_context(tc.tile_pool(name="ring2", bufs=2))
-        ring3 = ctx.enter_context(tc.tile_pool(name="ring3", bufs=3))
+        ring3 = ctx.enter_context(tc.tile_pool(name="ring3", bufs=4))
+        shared = ctx.enter_context(tc.tile_pool(name="shared", bufs=1))
         psum = ctx.enter_context(tc.psum_pool(name="psum", bufs=8))
 
         def kept(shape, dtype, name, tag=None):
@@ -42,44 +43,57 @@ def tile_list_melt_track_porosity_kernel(
         offs2_sb = lists.tile([P, PL // 16], U16, name="offs2_sb")
         pos1_sb = lists.tile([P, PL // 16], U16, name="pos1_sb")
 
-        tabw = [kept([P, T], I32, "tabw%d" % a) for a in range(2)]
+        tabw = [kept([P, T], I32, "tabw0"), shared.tile([P, T], I32, name="tabw1", offset=0, align_bytes=64)]
         tabs = kept([P, T], U8, "tabs")
         tab2w = kept([P, TB], I32, "tab2w")
         tab2s = kept([P, TB], U8, "tab2s")
         w2w_raw = kept([P, 2 * H], U8, "w2w_raw")
         w2s_raw = kept([P, H], U8, "w2s_raw")
         w2w = kept([P, 2 * H], U8, "w2w")
-        w2s = kept([P, H], U8, "w2s")
-        wgs0 = kept([P, 1, PL], F32, "wgs0")
-        wgs1 = kept([P, 1, PL], F32, "wgs1")
-        wgs23 = kept([P, 2, PL], F32, "wgs23")
-        wgs_rows = wgs.rearrange("(m t) j -> m t j", t=PACK)
+        w2s_first = kept([P, 2, P], U8, "w2s_first")
+        w2s_rest = kept([P, 2, PACK - 1, P], U8, "w2s")
+        wgs_raw = kept([P, PL], F32, "wgs_raw")
+        ident = kept([P, P], F32, "ident")
         bias_sb = kept([P, 2, PACK], F32, "bias_sb")
         gain_sb = kept([P, 2, PACK], F32, "gain_sb")
         pages = []
         warm = kept([P, 2], F32, "warm")
 
-        nc.vector.memset(w2s_raw[:].bitcast(I32), 0)
-        nc.gpsimd.memset(tab2s[:].bitcast(I32), 0)
+        nc.vector.memset(tab2s[:].bitcast(I32), 0)
+        nc.gpsimd.memset(w2s_raw[:].bitcast(I32), 0)
         nc.vector.memset(warm[:], 1.0)
+        make_identity(nc, ident[:])
         nc.gpsimd.memset(tabs[:].bitcast(I32), 0)
         nc.scalar.activation(warm[:, 1:2], warm[:, 0:1], ACT.Abs_reciprocal_sqrt)
 
         nc.sync.dma_start(offs2_sb[:], offs2)
         nc.sync.dma_start(w2w_raw[:].bitcast(I32), w2_words[0].bitcast(I32))
-        nc.sync.dma_start(bias_sb[:], bias.rearrange("(g p t) -> p g t", g=2, t=PACK))
-        for q in range(4):
-            nc.sync.dma_start(w2s_raw[32 * q : 32 * q + 4, :].bitcast(I32), w2_scales[0, 4 * q : 4 * q + 4, :].bitcast(I32))
-        nc.sync.dma_start(tab2w[:], tab2_words[0].rearrange("p t i -> p (t i)").bitcast(I32))
+        nc.sync.dma_start(wgs_raw[:], wgs)
         for q in range(4):
             nc.sync.dma_start(tab2s[32 * q : 32 * q + 4, :].bitcast(I32), tab2_scales[0, 4 * q : 4 * q + 4, :].bitcast(I32))
+        nc.sync.dma_start(tab2w[:], tab2_words[0].rearrange("p t i -> p (t i)").bitcast(I32))
+        for q in range(4):
+            nc.sync.dma_start(w2s_raw[32 * q : 32 * q + 4, :].bitcast(I32), w2_scales[0, 4 * q : 4 * q + 4, :].bitcast(I32))
         nc.sync.dma_start(pos1_sb[:], pos1)
+        nc.sync.dma_start(bias_sb[:], bias.rearrange("(g p t) -> p g t", g=2, t=PACK))
 
-        def load_wgs(tile, t0, t1):
-            for q in (0, 2, 1, 3):
-                nc.sync.dma_start(tile[32 * q : 32 * q + 32], wgs_rows[:, t0:t1, :])
-
-        load_wgs(wgs0, 0, 1)
+        turned = psum.tile([P, PL], F32, name="turned", tag="bank")
+        for c in range(PL // P):
+            nc.tensor.transpose(turned[:, P * c : P * (c + 1)], wgs_raw[:, P * c : P * (c + 1)], ident[:])
+        wgs_t = kept([P, PACK, PL], F32, "wgs_t", tag="sq")
+        dealt = []
+        for t in range(PACK):
+            nc.scalar.copy(
+                wgs_t[:, t, :].rearrange("p (c q m) -> p c q m", q=4, m=32),
+                turned[:].rearrange("p (c m t) -> p t c m", t=PACK, m=32)[:, t].unsqueeze(2).broadcast_to([P, PL // P, 4, 32]),
+            )
+            bank = psum.tile([P, PL], F32, name="dealt", tag="bank")
+            for c in range(PL // P):
+                nc.tensor.transpose(bank[:, P * c : P * (c + 1)], wgs_t[:, t, P * c : P * (c + 1)], ident[:])
+            dealt.append(bank)
+        wgs01 = kept([P, 2, PL], F32, "wgs01")
+        for t in range(2):
+            nc.scalar.copy(wgs01[:, t, :], dealt[t][:])
 
         def load_table(a):
             nc.sync.dma_start(tabw[a][:], tab_words[a].rearrange("p t i -> p (t i)").bitcast(I32))
@@ -97,7 +111,7 @@ def tile_list_melt_track_porosity_kernel(
 
         def prepare_w1(a, g):
             raw = load_rows(w1[PASS * a : PASS * (a + 1), PASS * g : PASS * (g + 1)], "w1raw")
-            grouped = ring2.tile([P, PACK * HALF], BF16, name="grouped", tag="grouped", align_bytes=64)
+            grouped = kept([P, PACK * HALF], BF16, "w1_grouped", tag=("u1_%d", "rs1_%d")[g] % a)
             for pair in range(2):
                 nc.scalar.copy(
                     grouped[:].rearrange("p (t m j) -> p m j t", t=PACK, j=PACK)[:, :, :, 2 * pair : 2 * pair + 2],
@@ -107,7 +121,7 @@ def tile_list_melt_track_porosity_kernel(
 
         def prepare_w3(g):
             raw = load_rows(w3[PASS * g : PASS * (g + 1), :], "w3raw")
-            grouped = ring2.tile([P, PACK * HALF], BF16, name="grouped", tag="grouped", align_bytes=64)
+            grouped = kept([P, PACK * HALF], BF16, "w3_grouped", tag=("u0", "z1")[g])
             nc.scalar.copy(
                 grouped[:].rearrange("p (c i t) -> p c t i", t=PACK, i=4),
                 raw[:].rearrange("p t (c i) -> p c t i", i=4),
@@ -118,14 +132,13 @@ def tile_list_melt_track_porosity_kernel(
             w2w[:].bitcast(U16).rearrange("p (g t m) -> p g t m", g=2, t=PACK),
             w2w_raw[:].bitcast(U16).rearrange("p (g m t) -> p g t m", g=2, t=PACK),
         )
-        nc.vector.tensor_copy(
-            w2s[:].rearrange("p (g t m) -> p g t m", g=2, t=PACK),
-            w2s_raw[:].rearrange("p (g m t) -> p g t m", g=2, t=PACK),
-        )
         v2 = kept([P, PL], U32, "v2")
         v2s = kept([P, PL], U8, "v2s")
-        nc.vector.tensor_copy(v2[:], tab2w[:].bitcast(U32).indirect(offs2_sb[:]))
         nc.vector.tensor_copy(v2s[:], tab2s[:].indirect(offs2_sb[:]))
+        nc.vector.tensor_copy(v2[:], tab2w[:].bitcast(U32).indirect(offs2_sb[:]))
+        w2s_dealt = w2s_raw[:].rearrange("p (g m t) -> p g t m", g=2, t=PACK)
+        nc.vector.tensor_copy(w2s_first[:], w2s_dealt[:, :, 0, :])
+        nc.vector.tensor_copy(w2s_rest[:], w2s_dealt[:, :, 1:PACK, :])
 
         b_sb = kept([P, 2 * PACK, PL], F32, "b_sb")
         order = (0, 4, 1, 5, 2, 3, 6, 7)
@@ -135,7 +148,7 @@ def tile_list_melt_track_porosity_kernel(
             nc.tensor.matmul_mx(
                 out=bank[:],
                 lhsT=w2w[:, 2 * P * n : 2 * P * (n + 1)].bitcast(FP4X4),
-                lhsT_scale=w2s[:, P * n : P * (n + 1)],
+                lhsT_scale=w2s_first[:, g, :] if t == 0 else w2s_rest[:, g, t - 1, :],
                 rhs=v2[:].bitcast(FP8X4),
                 rhs_scale=v2s[:],
                 start=True,
@@ -143,45 +156,47 @@ def tile_list_melt_track_porosity_kernel(
             )
             nc.scalar.activation(b_sb[:, n, :], bank[:], ACT.Identity, bias=bias_sb[:, g, t : t + 1])
 
-        for name in ("w2w_raw", "w2s_raw", "tab2w", "tab2s", "v2", "w2w", "w2s", "v2s"):
+        for name in ("w2w_raw", "tab2s", "tab2w", "w2s_raw", "v2", "w2w", "w2s", "v2s"):
             page = kept([P, S], F32, "page_" + name, tag=name)
             nc.gpsimd.memset(page[:], 0.0)
             pages.append(page)
         page_of = {n: pages[i] for i, n in enumerate(order)}
 
-        def place(n):
+        def place(n, weights):
             t = n % PACK
-            weight = (wgs0[:, 0, :], wgs1[:, 0, :], wgs23[:, 0, :], wgs23[:, 1, :])[t]
-            nc.vector.tensor_tensor(page_of[n][:].indirect(pos1_sb[:]), b_sb[:, n, :], weight, ALU.mult)
+            nc.vector.tensor_tensor(page_of[n][:].indirect(pos1_sb[:]), b_sb[:, n, :], weights[:, t % 2, :], ALU.mult)
 
-        place(0)
-        place(4)
+        place(0, wgs01)
+        place(4, wgs01)
 
         load_table(0)
         nc.sync.dma_start(offs_sb[:], offs)
-        for q in range(4):
-            nc.sync.dma_start(tabs[32 * q : 32 * q + 8, :].bitcast(I32), tab_scales[:, 4 * q : 4 * q + 4, :].bitcast(I32))
-        load_wgs(wgs1, 1, 2)
         v0 = kept([P, S], U32, "v0")
-        vs = kept([P, S], U8, "vs")
         nc.vector.tensor_copy(v0[:], tabw[0][:].bitcast(U32).indirect(offs_sb[:]))
-        nc.vector.tensor_copy(vs[:], tabs[:].indirect(offs_sb[:]))
         w1q = {}
         for g in range(2):
             for a in range(2):
                 w1q[a, g] = prepare_w1(a, g)
-        place(1)
-        place(5)
+        w3q = [prepare_w3(0)]
+        place(1, wgs01)
+        place(5, wgs01)
+        for q in range(4):
+            nc.sync.dma_start(tabs[32 * q : 32 * q + 8, :].bitcast(I32), tab_scales[:, 4 * q : 4 * q + 4, :].bitcast(I32))
         load_table(1)
         nc.sync.dma_start(gain_sb[:], gain.rearrange("(g p t) -> p g t", g=2, t=PACK))
         v1 = [kept([P, HALF], U32, "v1_%d" % h) for h in range(2)]
+        vs = [shared.tile([P, HALF], U8, name="vs_%d" % h, offset=HALF * h, align_bytes=64) for h in range(2)]
         for h in range(2):
             nc.vector.tensor_copy(v1[h][:], tabw[1][:].bitcast(U32).indirect(offs_sb[:, 32 * h : 32 * (h + 1)]))
-        load_wgs(wgs23, 2, 4)
+        for h in range(2):
+            nc.vector.tensor_copy(vs[h][:], tabs[:].indirect(offs_sb[:, 32 * h : 32 * (h + 1)]))
+        wgs23 = shared.tile([P, 2, PL], F32, name="wgs23", offset=S, align_bytes=64)
+        for t in range(2):
+            nc.scalar.copy(wgs23[:, t, :], dealt[2 + t][:])
 
-        def features(g, h, u, rs):
+        def features(g, h, u, rs, width=HALF):
             cols = slice(HALF * h, HALF * (h + 1))
-            sq = kept([P, PACK, HALF], F32, "sq", tag="tabw1")
+            sq = kept([P, PACK, HALF], F32, "sq")
             for t in range(PACK):
                 bank = psum.tile([P, HALF], F32, name="bank_y", tag="bank")
                 for a in range(2):
@@ -192,14 +207,15 @@ def tile_list_melt_track_porosity_kernel(
                         lhsT=codes[:, P * t : P * (t + 1)].bitcast(FP8X4),
                         lhsT_scale=scales[:, P * t : P * (t + 1)],
                         rhs=moving.bitcast(FP8X4),
-                        rhs_scale=vs[4 * a : P, cols],
+                        rhs_scale=vs[h][4 * a : P, :],
                         start=(a == 0),
                         stop=(a == 1),
                     )
                 gain_col = gain_sb[:, g, t : t + 1]
                 nc.scalar.activation(sq[:, t, :], bank[:], ACT.Square)
                 nc.scalar.activation(u[:, t, :], sq[:, t, :], ACT.Identity, bias=gain_col, scale=gain_col)
-            nc.scalar.activation(rs, sq[:], ACT.Abs_reciprocal_sqrt, bias=1.0)
+            for c0 in range(0, HALF, width):
+                nc.scalar.activation(rs[:, :, c0 : c0 + width], sq[:, :, c0 : c0 + width], ACT.Abs_reciprocal_sqrt, bias=1.0)
 
         def add_placed(g, u, cols):
             for t in range(PACK):
@@ -242,7 +258,7 @@ def tile_list_melt_track_porosity_kernel(
                     nc.sync.dma_start(out_rows[:, nt - 1 : nt + 1, c0 : c0 + width], pair.rearrange("p (a b) -> p a b", a=2))
 
         for n in (2, 3, 6, 7):
-            place(n)
+            place(n, wgs23)
         u0 = kept([P, PACK, S], F32, "u0")
         rs0 = kept([P, PACK, S], F32, "rs0", tag="tabw0")
         for h in range(2):
@@ -250,15 +266,15 @@ def tile_list_melt_track_porosity_kernel(
             features(0, h, u0[:, :, cols], rs0[:, :, cols])
         add_placed(0, u0[:], slice(0, S))
         z0 = quantise_z(u0[:], rs0[:], S, "z0", "z0")
-        w3q = [prepare_w3(g) for g in range(2)]
+        w3q.append(prepare_w3(1))
         u1 = [kept([P, PACK, HALF], F32, "u1_%d" % h) for h in range(2)]
         rs1 = [kept([P, PACK, HALF], F32, "rs1_%d" % h) for h in range(2)]
         features(1, 0, u1[0][:], rs1[0][:])
         add_placed(1, u1[0][:], slice(0, HALF))
         z10 = quantise_z(u1[0][:], rs1[0][:], HALF, "z10", "z1")
-        features(1, 1, u1[1][:], rs1[1][:])
+        features(1, 1, u1[1][:], rs1[1][:], 256)
         add_placed(1, u1[1][:], slice(HALF, S))
-        staged0 = kept([P, PACK * HALF], F32, "staged0", tag="tabw1")
+        staged0 = kept([P, PACK * HALF], F32, "staged0", tag="sq")
         staged1 = kept([P, 2, PACK * 256], F32, "staged1", tag="tabw0")
         z11 = []
         for k in range(2):

@@ -32,7 +32,6 @@ def tile_list_melt_track_porosity_kernel(
     with ExitStack() as ctx:
         lists = ctx.enter_context(tc.tile_pool(name="lists", bufs=1))
         keep = ctx.enter_context(tc.tile_pool(name="keep", bufs=1))
-        ring3 = ctx.enter_context(tc.tile_pool(name="ring3", bufs=4))
         shared = ctx.enter_context(tc.tile_pool(name="shared", bufs=1))
         psum = ctx.enter_context(tc.psum_pool(name="psum", bufs=8))
 
@@ -44,7 +43,7 @@ def tile_list_melt_track_porosity_kernel(
         pos1_sb = lists.tile([P, PL // 16], U16, name="pos1_sb")
 
         tabw = [kept([P, T], I32, "tabw0"), shared.tile([P, T], I32, name="tabw1", offset=0, align_bytes=64)]
-        tabs = kept([P, T], U8, "tabs")
+        tabs = shared.tile([P, T], U8, name="tabs", offset=4 * T, align_bytes=64)
         tab2w = kept([P, TB], I32, "tab2w")
         tab2s = kept([P, TB], U8, "tab2s")
         w2w_raw = kept([P, 2 * H], U8, "w2w_raw")
@@ -56,12 +55,14 @@ def tile_list_melt_track_porosity_kernel(
         ident = kept([P, P], F32, "ident")
         bias_sb = kept([P, 2, PACK], F32, "bias_sb")
         gain_sb = kept([P, 2, PACK], F32, "gain_sb")
-        pages = []
+        pages = [kept([P, S], F32, "page%d" % i) for i in range(2)]
         warm = kept([P, 2], F32, "warm")
 
         nc.vector.memset(tab2s[:].bitcast(I32), 0)
         nc.gpsimd.memset(w2s_raw[:].bitcast(I32), 0)
         nc.vector.memset(warm[:], 1.0)
+        for page in pages:
+            nc.vector.memset(page[:], 0.0)
         make_identity(nc, ident[:])
         nc.gpsimd.memset(tabs[:].bitcast(I32), 0)
         nc.scalar.activation(warm[:, 1:2], warm[:, 0:1], ACT.Abs_reciprocal_sqrt)
@@ -98,35 +99,37 @@ def tile_list_melt_track_porosity_kernel(
         def load_table(a):
             nc.sync.dma_start(tabw[a][:], tab_words[a].rearrange("p t i -> p (t i)").bitcast(I32))
 
-        def load_rows(rows, name):
-            raw = ring3.tile([P, PACK, HALF], F32, name=name, tag="raw")
+        def load_rows(rows, name, tag):
+            raw = kept([P, PACK, rows.shape[1]], F32, name, tag=tag)
             nc.sync.dma_start(raw[:], rows.rearrange("(p j) c -> p j c", j=PACK))
             return raw
 
-        def quantise(grouped, name, width=HALF):
-            codes = kept([P, width], U32, name + "_codes")
+        def quantise(grouped, name, width=HALF, codes=None):
+            if codes is None:
+                codes = kept([P, width], U32, name + "_codes")
             scales = kept([P, width], U8, name + "_scales")
             nc.vector.quantize_mx(out=codes[:].bitcast(FP8X4), scales=scales[:], in_=grouped[:])
             return codes, scales
 
-        def prepare_w1(a, g):
-            raw = load_rows(w1[PASS * a : PASS * (a + 1), PASS * g : PASS * (g + 1)], "w1raw")
-            grouped = kept([P, PACK * HALF], BF16, "w1_grouped", tag=("u1_%d", "rs1_%d")[g] % a)
-            for pair in range(2):
-                nc.scalar.copy(
-                    grouped[:].rearrange("p (t m j) -> p m j t", t=PACK, j=PACK)[:, :, :, 2 * pair : 2 * pair + 2],
-                    raw[:].rearrange("p j (m t) -> p m j t", t=PACK)[:, :, :, 2 * pair : 2 * pair + 2],
-                )
-            return quantise(grouped, "w1_%d%d" % (a, g))
+        def prepare_w1(a):
+            raw = load_rows(w1[PASS * a : PASS * (a + 1), :], "w1raw", "raw%d" % a)
+            for g in range(2):
+                grouped = kept([P, PACK * HALF], BF16, "w1_grouped", tag=("u1_%d", "rs1_%d")[g] % a)
+                for pair in range(2):
+                    nc.scalar.copy(
+                        grouped[:].rearrange("p (t m j) -> p m j t", t=PACK, j=PACK)[:, :, :, 2 * pair : 2 * pair + 2],
+                        raw[:, :, PASS * g : PASS * (g + 1)].rearrange("p j (m t) -> p m j t", t=PACK)[:, :, :, 2 * pair : 2 * pair + 2],
+                    )
+                w1q[a, g] = quantise(grouped, "w1_%d%d" % (a, g))
 
-        def prepare_w3(g):
-            raw = load_rows(w3[PASS * g : PASS * (g + 1), :], "w3raw")
+        def group_w3(g):
+            raw = load_rows(w3[PASS * g : PASS * (g + 1), :], "w3raw", ("z0", "raw0")[g])
             grouped = kept([P, PACK * HALF], BF16, "w3_grouped", tag=("u0", "z1")[g])
             nc.scalar.copy(
                 grouped[:].rearrange("p (c i t) -> p c t i", t=PACK, i=4),
                 raw[:].rearrange("p t (c i) -> p c t i", i=4),
             )
-            return quantise(grouped, "w3_%d" % g)
+            return grouped
 
         nc.vector.tensor_copy(
             w2w[:].bitcast(U16).rearrange("p (g t m) -> p g t m", g=2, t=PACK),
@@ -156,7 +159,7 @@ def tile_list_melt_track_porosity_kernel(
             )
             nc.scalar.activation(b_sb[:, n, :], bank[:], ACT.Identity, bias=bias_sb[:, g, t : t + 1])
 
-        for name in ("w2w_raw", "tab2s", "tab2w", "w2s_raw", "v2", "w2w", "w2s", "v2s"):
+        for name in ("w2s_raw", "w2s_first", "v2", "w2w", "w2s", "v2s"):
             page = kept([P, S], F32, "page_" + name, tag=name)
             nc.gpsimd.memset(page[:], 0.0)
             pages.append(page)
@@ -174,15 +177,14 @@ def tile_list_melt_track_porosity_kernel(
         v0 = kept([P, S], U32, "v0")
         nc.vector.tensor_copy(v0[:], tabw[0][:].bitcast(U32).indirect(offs_sb[:]))
         w1q = {}
-        for g in range(2):
-            for a in range(2):
-                w1q[a, g] = prepare_w1(a, g)
-        w3q = [prepare_w3(0)]
+        for a in range(2):
+            prepare_w1(a)
+        w3_grouped = group_w3(0)
         place(1, wgs01)
         place(5, wgs01)
+        load_table(1)
         for q in range(4):
             nc.sync.dma_start(tabs[32 * q : 32 * q + 8, :].bitcast(I32), tab_scales[:, 4 * q : 4 * q + 4, :].bitcast(I32))
-        load_table(1)
         nc.sync.dma_start(gain_sb[:], gain.rearrange("(g p t) -> p g t", g=2, t=PACK))
         v1 = [kept([P, HALF], U32, "v1_%d" % h) for h in range(2)]
         vs = [shared.tile([P, HALF], U8, name="vs_%d" % h, offset=HALF * h, align_bytes=64) for h in range(2)]
@@ -190,7 +192,9 @@ def tile_list_melt_track_porosity_kernel(
             nc.vector.tensor_copy(v1[h][:], tabw[1][:].bitcast(U32).indirect(offs_sb[:, 32 * h : 32 * (h + 1)]))
         for h in range(2):
             nc.vector.tensor_copy(vs[h][:], tabs[:].indirect(offs_sb[:, 32 * h : 32 * (h + 1)]))
-        wgs23 = shared.tile([P, 2, PL], F32, name="wgs23", offset=S, align_bytes=64)
+        w3_codes = shared.tile([P, HALF], U32, name="w3_codes", offset=4 * T + T // 2, align_bytes=64)
+        w3q = [quantise(w3_grouped, "w3_0", codes=w3_codes)]
+        wgs23 = shared.tile([P, 2, PL], F32, name="wgs23", offset=4 * T - T // 2, align_bytes=64)
         for t in range(2):
             nc.scalar.copy(wgs23[:, t, :], dealt[2 + t][:])
 
@@ -211,8 +215,9 @@ def tile_list_melt_track_porosity_kernel(
                         start=(a == 0),
                         stop=(a == 1),
                     )
-                gain_col = gain_sb[:, g, t : t + 1]
                 nc.scalar.activation(sq[:, t, :], bank[:], ACT.Square)
+            for t in range(PACK):
+                gain_col = gain_sb[:, g, t : t + 1]
                 nc.scalar.activation(u[:, t, :], sq[:, t, :], ACT.Identity, bias=gain_col, scale=gain_col)
             for c0 in range(0, HALF, width):
                 nc.scalar.activation(rs[:, :, c0 : c0 + width], sq[:, :, c0 : c0 + width], ACT.Abs_reciprocal_sqrt, bias=1.0)
@@ -224,9 +229,9 @@ def tile_list_melt_track_porosity_kernel(
         def quantise_z(u, rs, width, name, tag):
             z = keep.tile([P, PACK * width], BF16, name="z", tag=tag, align_bytes=64)
             nc.vector.tensor_tensor(
-                z[:].rearrange("p (c i t) -> p c t i", t=PACK, i=4),
-                u.rearrange("p t (c i) -> p c t i", i=4),
-                rs.rearrange("p t (c i) -> p c t i", i=4),
+                z[:].rearrange("p (c i t) -> p c t i", t=PACK, i=2),
+                u.rearrange("p t (c i) -> p c t i", i=2),
+                rs.rearrange("p t (c i) -> p c t i", i=2),
                 ALU.mult,
             )
             return quantise(z, name, width)
@@ -266,7 +271,7 @@ def tile_list_melt_track_porosity_kernel(
             features(0, h, u0[:, :, cols], rs0[:, :, cols])
         add_placed(0, u0[:], slice(0, S))
         z0 = quantise_z(u0[:], rs0[:], S, "z0", "z0")
-        w3q.append(prepare_w3(1))
+        w3q.append(quantise(group_w3(1), "w3_1"))
         u1 = [kept([P, PACK, HALF], F32, "u1_%d" % h) for h in range(2)]
         rs1 = [kept([P, PACK, HALF], F32, "rs1_%d" % h) for h in range(2)]
         features(1, 0, u1[0][:], rs1[0][:])

from contextlib import ExitStack

import concourse.mybir as mybir
from concourse.masks import make_identity

K, K2, H, N, T, TB, S, PL = 1024, 512, 1024, 512, 4096, 2048, 1024, 512
FLOPS = 2 * (K * H * S + K2 * H * PL + H * N * S)

F32 = mybir.dt.float32
BF16 = mybir.dt.bfloat16
I32 = mybir.dt.int32
U32 = mybir.dt.uint32
U16 = mybir.dt.uint16
U8 = mybir.dt.uint8
FP8X4 = mybir.dt.float8_e4m3fn_x4
FP4X4 = mybir.dt.float4_e2m1fn_x4
ALU = mybir.AluOpType
ACT = mybir.ActivationFunctionType

P = 128
PACK = 4
PASS = P * PACK
HALF = 512
EARLY = 3


def tile_list_melt_track_porosity_kernel(
    tc, tab_words, tab_scales, tab2_words, tab2_scales, offs, offs2, pos1,
    w1, w2_words, w2_scales, bias, wgs, gain, w3, out,
):
    nc = tc.nc
    with ExitStack() as ctx:
        lists = ctx.enter_context(tc.tile_pool(name="lists", bufs=1))
        keep = ctx.enter_context(tc.tile_pool(name="keep", bufs=1))
        shared = ctx.enter_context(tc.tile_pool(name="shared", bufs=1))
        psum = ctx.enter_context(tc.psum_pool(name="psum", bufs=8))

        def kept(shape, dtype, name, tag=None):
            return keep.tile(shape, dtype, name=name, tag=tag or name, align_bytes=64)

        offs_sb = lists.tile([P, S // 16], U16, name="offs_sb")
        offs2_sb = lists.tile([P, PL // 16], U16, name="offs2_sb")
        pos1_sb = lists.tile([P, PL // 16], U16, name="pos1_sb")

        tabw = [kept([P, T], I32, "tabw0"), shared.tile([P, T], I32, name="tabw1", offset=0, align_bytes=64)]
        tabs = shared.tile([P, T], U8, name="tabs", offset=4 * T, align_bytes=64)
        tab2w = kept([P, TB], I32, "tab2w")
        tab2s = kept([P, TB], U8, "tab2s")
        w2w_raw = kept([P, 2 * H], U8, "w2w_raw")
        w2s_raw = kept([P, H], U8, "w2s_raw")
        w2w = kept([P, 2 * H], U8, "w2w")
        w2s_first = kept([P, 2, P], U8, "w2s_first")
        w2s_rest = kept([P, 2, PACK - 1, P], U8, "w2s")
        wgs_raw = kept([P, PL], F32, "wgs_raw")
        ident = kept([P, P], F32, "ident")
        bias_sb = kept([P, 2, PACK], F32, "bias_sb")
        gain_sb = kept([P, 2, PACK], F32, "gain_sb")
        pages = [kept([P, S], F32, "page%d" % i) for i in range(2)]
        warm = kept([P, 2], F32, "warm")

        nc.vector.memset(tab2s[:].bitcast(I32), 0)
        nc.gpsimd.memset(w2s_raw[:].bitcast(I32), 0)
        nc.vector.memset(warm[:], 1.0)
        for page in pages:
            nc.vector.memset(page[:], 0.0)
        make_identity(nc, ident[:])
        nc.gpsimd.memset(tabs[:].bitcast(I32), 0)
        nc.scalar.activation(warm[:, 1:2], warm[:, 0:1], ACT.Abs_reciprocal_sqrt)

        nc.sync.dma_start(offs2_sb[:], offs2)
        nc.sync.dma_start(w2w_raw[:].bitcast(I32), w2_words[0].bitcast(I32))
        nc.sync.dma_start(wgs_raw[:], wgs)
        for q in range(4):
            nc.sync.dma_start(tab2s[32 * q : 32 * q + 4, :].bitcast(I32), tab2_scales[0, 4 * q : 4 * q + 4, :].bitcast(I32))
        nc.sync.dma_start(tab2w[:], tab2_words[0].rearrange("p t i -> p (t i)").bitcast(I32))
        for q in range(4):
            nc.sync.dma_start(w2s_raw[32 * q : 32 * q + 4, :].bitcast(I32), w2_scales[0, 4 * q : 4 * q + 4, :].bitcast(I32))
        nc.sync.dma_start(pos1_sb[:], pos1)
        nc.sync.dma_start(bias_sb[:], bias.rearrange("(g p t) -> p g t", g=2, t=PACK))

        turned = psum.tile([P, PL], F32, name="turned", tag="bank")
        for c in range(PL // P):
            nc.tensor.transpose(turned[:, P * c : P * (c + 1)], wgs_raw[:, P * c : P * (c + 1)], ident[:])
        wgs_t = kept([P, PACK, PL], F32, "wgs_t", tag="sq")
        dealt = []
        for t in range(PACK):
            nc.scalar.copy(
                wgs_t[:, t, :].rearrange("p (c q m) -> p c q m", q=4, m=32),
                turned[:].rearrange("p (c m t) -> p t c m", t=PACK, m=32)[:, t].unsqueeze(2).broadcast_to([P, PL // P, 4, 32]),
            )
            bank = psum.tile([P, PL], F32, name="dealt", tag="bank")
            for c in range(PL // P):
                nc.tensor.transpose(bank[:, P * c : P * (c + 1)], wgs_t[:, t, P * c : P * (c + 1)], ident[:])
            dealt.append(bank)
        wgs01 = kept([P, 2, PL], F32, "wgs01")
        for t in range(2):
            nc.scalar.copy(wgs01[:, t, :], dealt[t][:])

        def load_table(a):
            nc.sync.dma_start(tabw[a][:], tab_words[a].rearrange("p t i -> p (t i)").bitcast(I32))

        def load_rows(rows, name, tag):
            raw = kept([P, PACK, rows.shape[1]], F32, name, tag=tag)
            nc.sync.dma_start(raw[:], rows.rearrange("(p j) c -> p j c", j=PACK))
            return raw

        def quantise(grouped, name, width=HALF, codes=None):
            if codes is None:
                codes = kept([P, width], U32, name + "_codes")
            scales = kept([P, width], U8, name + "_scales")
            nc.vector.quantize_mx(out=codes[:].bitcast(FP8X4), scales=scales[:], in_=grouped[:])
            return codes, scales

        def prepare_w1(a):
            raw = load_rows(w1[PASS * a : PASS * (a + 1), :], "w1raw", "raw%d" % a)
            for g in range(2):
                grouped = kept([P, PACK * HALF], BF16, "w1_grouped", tag=("u1_%d", "rs1_%d")[g] % a)
                for pair in range(2):
                    nc.scalar.copy(
                        grouped[:].rearrange("p (t m j) -> p m j t", t=PACK, j=PACK)[:, :, :, 2 * pair : 2 * pair + 2],
                        raw[:, :, PASS * g : PASS * (g + 1)].rearrange("p j (m t) -> p m j t", t=PACK)[:, :, :, 2 * pair : 2 * pair + 2],
                    )
                w1q[a, g] = quantise(grouped, "w1_%d%d" % (a, g))

        def group_w3(g):
            raw = load_rows(w3[PASS * g : PASS * (g + 1), :], "w3raw", ("z0", "raw0")[g])
            grouped = kept([P, PACK * HALF], BF16, "w3_grouped", tag=("u0", "z1")[g])
            nc.scalar.copy(
                grouped[:].rearrange("p (c i t) -> p c t i", t=PACK, i=4),
                raw[:].rearrange("p t (c i) -> p c t i", i=4),
            )
            return grouped

        nc.vector.tensor_copy(
            w2w[:].bitcast(U16).rearrange("p (g t m) -> p g t m", g=2, t=PACK),
            w2w_raw[:].bitcast(U16).rearrange("p (g m t) -> p g t m", g=2, t=PACK),
        )
        v2 = kept([P, PL], U32, "v2")
        v2s = kept([P, PL], U8, "v2s")
        nc.vector.tensor_copy(v2s[:], tab2s[:].indirect(offs2_sb[:]))
        nc.vector.tensor_copy(v2[:], tab2w[:].bitcast(U32).indirect(offs2_sb[:]))
        w2s_dealt = w2s_raw[:].rearrange("p (g m t) -> p g t m", g=2, t=PACK)
        nc.vector.tensor_copy(w2s_first[:], w2s_dealt[:, :, 0, :])
        nc.vector.tensor_copy(w2s_rest[:], w2s_dealt[:, :, 1:PACK, :])

        b_sb = kept([P, 2 * PACK, PL], F32, "b_sb")
        order = (0, 4, 1, 5, 2, 3, 6, 7)
        for n in order:
            g, t = divmod(n, PACK)
            bank = psum.tile([P, PL], F32, name="bank_b", tag="bank")
            nc.tensor.matmul_mx(
                out=bank[:],
                lhsT=w2w[:, 2 * P * n : 2 * P * (n + 1)].bitcast(FP4X4),
                lhsT_scale=w2s_first[:, g, :] if t == 0 else w2s_rest[:, g, t - 1, :],
                rhs=v2[:].bitcast(FP8X4),
                rhs_scale=v2s[:],
                start=True,
                stop=True,
            )
            nc.scalar.activation(b_sb[:, n, :], bank[:], ACT.Identity, bias=bias_sb[:, g, t : t + 1])

        for name in ("w2s_raw", "w2s_first", "v2", "w2w", "w2s", "v2s"):
            page = kept([P, S], F32, "page_" + name, tag=name)
            nc.gpsimd.memset(page[:], 0.0)
            pages.append(page)
        page_of = {n: pages[i] for i, n in enumerate(order)}

        def place(n, weights):
            t = n % PACK
            nc.vector.tensor_tensor(page_of[n][:].indirect(pos1_sb[:]), b_sb[:, n, :], weights[:, t % 2, :], ALU.mult)

        place(0, wgs01)
        place(4, wgs01)

        load_table(0)
        nc.sync.dma_start(offs_sb[:], offs)
        v0 = kept([P, S], U32, "v0")
        nc.vector.tensor_copy(v0[:], tabw[0][:].bitcast(U32).indirect(offs_sb[:]))
        w1q = {}
        for a in range(2):
            prepare_w1(a)
        w3_grouped = group_w3(0)
        place(1, wgs01)
        place(5, wgs01)
        load_table(1)
        for q in range(4):
            nc.sync.dma_start(tabs[32 * q : 32 * q + 8, :].bitcast(I32), tab_scales[:, 4 * q : 4 * q + 4, :].bitcast(I32))
        nc.sync.dma_start(gain_sb[:], gain.rearrange("(g p t) -> p g t", g=2, t=PACK))
        v1 = [kept([P, HALF], U32, "v1_%d" % h) for h in range(2)]
        vs = [shared.tile([P, HALF], U8, name="vs_%d" % h, offset=HALF * h, align_bytes=64) for h in range(2)]
        for h in range(2):
            nc.vector.tensor_copy(v1[h][:], tabw[1][:].bitcast(U32).indirect(offs_sb[:, 32 * h : 32 * (h + 1)]))
        for h in range(2):
            nc.vector.tensor_copy(vs[h][:], tabs[:].indirect(offs_sb[:, 32 * h : 32 * (h + 1)]))
        w3_codes = shared.tile([P, HALF], U32, name="w3_codes", offset=4 * T + T // 2, align_bytes=64)
        w3q = [quantise(w3_grouped, "w3_0", codes=w3_codes)]
        wgs23 = shared.tile([P, 2, PL], F32, name="wgs23", offset=4 * T - T // 2, align_bytes=64)
        for t in range(2):
            nc.scalar.copy(wgs23[:, t, :], dealt[2 + t][:])

        def features(g, h, u, rs, width=HALF):
            cols = slice(HALF * h, HALF * (h + 1))
            sq = kept([P, PACK, HALF], F32, "sq")
            for t in range(PACK):
                bank = psum.tile([P, HALF], F32, name="bank_y", tag="bank")
                for a in range(2):
                    codes, scales = w1q[a, g]
                    moving = v0[:, cols] if a == 0 else v1[h][:]
                    nc.tensor.matmul_mx(
                        out=bank[:],
                        lhsT=codes[:, P * t : P * (t + 1)].bitcast(FP8X4),
                        lhsT_scale=scales[:, P * t : P * (t + 1)],
                        rhs=moving.bitcast(FP8X4),
                        rhs_scale=vs[h][4 * a : P, :],
                        start=(a == 0),
                        stop=(a == 1),
                    )
                nc.scalar.activation(sq[:, t, :], bank[:], ACT.Square)
            for t in range(PACK):
                gain_col = gain_sb[:, g, t : t + 1]
                nc.scalar.activation(u[:, t, :], sq[:, t, :], ACT.Identity, bias=gain_col, scale=gain_col)
            for c0 in range(0, HALF, width):
                nc.scalar.activation(rs[:, :, c0 : c0 + width], sq[:, :, c0 : c0 + width], ACT.Abs_reciprocal_sqrt, bias=1.0)

        def add_placed(g, u, cols):
            for t in range(PACK):
                nc.vector.tensor_tensor(u[:, t, :], u[:, t, :], page_of[PACK * g + t][:, cols], ALU.add)

        def quantise_z(u, rs, width, name, tag):
            z = keep.tile([P, PACK * width], BF16, name="z", tag=tag, align_bytes=64)
            nc.vector.tensor_tensor(
                z[:].rearrange("p (c i t) -> p c t i", t=PACK, i=2),
                u.rearrange("p t (c i) -> p c t i", i=2),
                rs.rearrange("p t (c i) -> p c t i", i=2),
                ALU.mult,
            )
            return quantise(z, name, width)

        out_rows = out.rearrange("(nt p) j -> p nt j", p=P)

        def project(c0, width, zq, flat, last):
            banks = [psum.tile([P, width], F32, name="bank_o", tag="bank") for nt in range(N // P)]
            for g in range(2):
                codes, scales = zq[g]
                for nt in range(N // P):
                    nc.tensor.matmul_mx(
                        out=banks[nt][:],
                        lhsT=w3q[g][0][:, P * nt : P * (nt + 1)].bitcast(FP8X4),
                        lhsT_scale=w3q[g][1][:, P * nt : P * (nt + 1)],
                        rhs=codes.bitcast(FP8X4),
                        rhs_scale=scales,
                        start=(g == 0),
                        stop=(g == 1),
                    )
            for nt in range(N // P):
                res = flat[:, width * nt : width * (nt + 1)]
                if last and nt >= 2:
                    nc.vector.tensor_copy(res, banks[nt][:])
                else:
                    nc.scalar.copy(res, banks[nt][:])
                if nt % 2 == 1:
                    pair = flat[:, width * (nt - 1) : width * (nt + 1)]
                    nc.sync.dma_start(out_rows[:, nt - 1 : nt + 1, c0 : c0 + width], pair.rearrange("p (a b) -> p a b", a=2))

        for n in (2, 3, 6, 7):
            place(n, wgs23)
        u0 = kept([P, PACK, S], F32, "u0")
        rs0 = kept([P, PACK, S], F32, "rs0", tag="tabw0")
        for h in range(2):
            cols = slice(HALF * h, HALF * (h + 1))
            features(0, h, u0[:, :, cols], rs0[:, :, cols])
        add_placed(0, u0[:], slice(0, S))
        z0 = quantise_z(u0[:], rs0[:], S, "z0", "z0")
        w3q.append(quantise(group_w3(1), "w3_1"))
        u1 = [kept([P, PACK, HALF], F32, "u1_%d" % h) for h in range(2)]
        rs1 = [kept([P, PACK, HALF], F32, "rs1_%d" % h) for h in range(2)]
        features(1, 0, u1[0][:], rs1[0][:])
        add_placed(1, u1[0][:], slice(0, HALF))
        z10 = quantise_z(u1[0][:], rs1[0][:], HALF, "z10", "z1")
        features(1, 1, u1[1][:], rs1[1][:], 256)
        add_placed(1, u1[1][:], slice(HALF, S))
        staged0 = kept([P, PACK * HALF], F32, "staged0", tag="sq")
        staged1 = kept([P, 2, PACK * 256], F32, "staged1", tag="tabw0")
        z11 = []
        for k in range(2):
            cols = slice(256 * k, 256 * (k + 1))
            z11.append(quantise_z(u1[1][:, :, cols], rs1[1][:, :, cols], 256, "z11_%d" % k, ("z0", "z1")[k]))
        project(0, HALF, ((z0[0][:, 0:HALF], z0[1][:, 0:HALF]), (z10[0][:], z10[1][:])), staged0[:], False)
        for k in range(2):
            cols = slice(HALF + 256 * k, HALF + 256 * (k + 1))
            project(HALF + 256 * k, 256, ((z0[0][:, cols], z0[1][:, cols]), (z11[k][0][:], z11[k][1][:])), staged1[:, k, :], k == 1)
